import numpy as np, ml_dtypes
CORES = [21,29,37,45,53,61,69,77,85]
N = 9
QP = 128
def setup_inputs(rng):
    m = 150 * rng.standard_normal((1, QP, 1), dtype=np.float32) + 3 * rng.standard_normal((N, QP, 1), dtype=np.float32)
    m = (m + rng.uniform(100, 300, (1, QP, 1)) * (rng.random((1, QP, 1)) < 0.7) * (rng.random((N, QP, 1)) < 0.5)).astype(np.float32)
    l = 20 * (1 + np.abs(rng.standard_normal((N, QP, 1), dtype=np.float32)))
    return {"o": (l * rng.standard_normal((N, QP, 128), dtype=np.float32) / 4).astype(ml_dtypes.bfloat16), "ml": np.concatenate([m, l], axis=2)}
def setup_inputs_big(rng):
    d = setup_inputs(rng)
    for k in ("o",): d[k] = (d[k].astype(np.float32) * 1048576.0).astype(d[k].dtype)
    return d
def setup_inputs_small(rng):
    d = setup_inputs(rng)
    for k in ("o",): d[k] = (d[k].astype(np.float32) * (1 / 1048576.0)).astype(d[k].dtype)
    return d
def setup_inputs_apart(rng):
    d = setup_inputs(rng)
    f = (10.0 ** rng.permutation(np.linspace(-1.5, 1.5, N))).astype(np.float32).reshape(N, 1, 1)
    for k in ("o",): d[k] = (d[k].astype(np.float32) * f).astype(d[k].dtype)
    return d
def reference(o, ml):
    O, ML = o.astype(np.float64), ml.astype(np.float64)
    m, l = ML[:, :, 0:1], ML[:, :, 1:2]
    f = np.exp(m - m.max(axis=0))
    y = ((f * O).sum(axis=0) / (f * l).sum(axis=0)).astype(ml_dtypes.bfloat16)
    return {"y": np.broadcast_to(y, (N,) + y.shape)}

@@ -1,0 +1,174 @@
+from concourse.bass import DstId, RemoteDMATransfer
+from concourse.mybir import AluOpType, AxisListType, ActivationFunctionType
+
+W = 136
+D = 128
+CL, CH, CLO = 128, 129, 130
+PAY = 131
+NPOS = 10
+
+SCRATCH = {
+    "land": ("sbuf", [128, NPOS * W], "bfloat16"),
+    "mlb": ("sbuf", [128, 2], "float32"),
+    "ones": ("sbuf", [128, 128], "bfloat16"),
+    "ident": ("sbuf", [128, 128], "bfloat16"),
+    "dg": ("sbuf", [128, NPOS * 128], "bfloat16"),
+    "nn": ("sbuf", [128, 12], "float32"),
+    "f": ("sbuf", [128, 16], "bfloat16"),
+    "fl": ("sbuf", [128, 12], "float32"),
+    "den": ("sbuf", [128, 4], "float32"),
+    "rden": ("sbuf", [128, 4], "float32"),
+    "ysb": ("sbuf", [128, 128], "bfloat16"),
+    "psa": ("psum", [128, 512], "float32"),
+    "psb": ("psum", [128, 512], "float32"),
+}
+SEMAPHORES = (["ldo", "ldm", "pk1", "pk2", "pk3", "one", "idn", "harr", "arra", "arrb", "sent", "st",
+               "va0", "va1", "vm0", "vm1", "ex0", "ex1", "pe0", "pe1", "ev0", "fls", "dns", "rcs", "yv"]
+              + ["d%d" % p for p in range(NPOS)])
+
+
+def _bits(mask):
+    return bin(mask).count("1")
+
+
+def _groups(ranks, topo, r):
+    near = [x for x in ranks if x == r or topo.may_write(x, r)]
+    far = [x for x in ranks if x not in near]
+    return near, far
+
+
+def _pos(ranks, topo, r, s):
+    near, far = _groups(ranks, topo, r)
+    return near.index(s) if s in near else len(near) + 1 + far.index(s)
+
+
+def _plan(ranks, topo, c):
+    i = ranks.index(c)
+    n = len(ranks)
+    turn = lambda d: (ranks.index(d) - i) % n
+    near = sorted([d for d in ranks if d != c and topo.may_write(c, d)], key=turn)
+    far = sorted([d for d in ranks if d != c and not topo.may_write(c, d)],
+                 key=lambda d: (topo.mates(topo.chip(c), topo.chip(d)), turn(d)))
+    cand = [x for x in range(topo.CORES_PER_CHIP * topo.CHIPS)
+            if topo.chip(x) == topo.chip(c) and x not in ranks and all(topo.may_write(x, d) for d in far)]
+    h1 = [x for x in cand if topo.die(x) == topo.die(c)][0]
+    h2 = [x for x in cand if topo.die(x) != topo.die(c)][0]
+    k = (len(far) + 1) // 2
+    return near, [(h1, far[:k]), (h2, far[k:])]
+
+
+def _send(g, T, topo, src_core, src_ap, dests, dst_aps, mask, remote_sem):
+    ids = []
+    for d in dests:
+        rid, pid, _se = topo.addr(d)
+        ids.append(DstId(rid=rid, pnc=pid))
+    g.remote_dma_fused([RemoteDMATransfer(dst_ids=ids, dma_engine_mask=mask, remote_sem=remote_sem,
+                                          srcs=[src_ap], dsts=dst_aps, alu_op=0)], local_sem=T.sem.sent)
+    return _bits(mask)
+
+
+def rank_program(g, core, T, topo):
+    ranks = list(T.cores)
+    land = T.land
+    S = T.sem
+    slot = lambda p, n: land[:, p * W:p * W + n]
+
+    if T.rank_of(core) is None:
+        for r in ranks:
+            if topo.chip(r) != topo.chip(core):
+                continue
+            for h, dests in _plan(ranks, topo, r)[1]:
+                if h != core:
+                    continue
+                inside = topo.mask(r, h) & ~topo.mask(r, dests[0])
+                g.wait_ge(S.harr, _bits(inside))
+                n = _send(g, T, topo, core, slot(0, PAY), dests,
+                          [slot(_pos(ranks, topo, d, r), PAY) for d in dests], topo.mask(core, dests[0]), S.arrb)
+                g.wait_ge(S.sent, n)
+        return
+
+    v, sc, pe, sy = g.vector, g.scalar, g.tensor, g.sync
+    near_in, far_in = _groups(ranks, topo, core)
+    na, nb = len(near_in), len(far_in)
+    own = _pos(ranks, topo, core, core)
+    near, helpers = _plan(ranks, topo, core)
+    col = lambda a, b, k: land[:, a * W + k:(b - 1) * W + k + 1:W]
+    one = lambda p, k: land[:, p * W + k:p * W + k + 1]
+
+    sy.dma_start(slot(own, D), T.o[:]).then_inc(S.ldo, 16)
+    sc.dma_start(T.mlb[:], T.ml[:]).then_inc(S.ldm, 16)
+    v.memset(T.ones[:], 1.0).then_inc(S.one, 1)
+    g.wait_ge(S.one, 1)
+    g.affine_select(T.ident[:], T.ones[:], [[-1, 128]], AluOpType.is_equal, 0.0, 0, 1).then_inc(S.idn, 1)
+
+    v.wait_ge(S.ldm, 16)
+    v.tensor_scalar(one(own, CH), T.mlb[:, 0:1], -1.0, None, AluOpType.mult).then_inc(S.pk1, 1)
+    v.tensor_copy(one(own, CL), T.mlb[:, 1:2]).then_inc(S.pk3, 1)
+    v.wait_ge(S.pk1, 1)
+    v.tensor_scalar(one(own, CLO), T.mlb[:, 0:1], -1.0, one(own, CH), AluOpType.mult,
+                    AluOpType.subtract).then_inc(S.pk2, 1)
+
+    g.wait_ge(S.ldo, 16)
+    g.wait_ge(S.pk3, 1)
+    g.wait_ge(S.pk2, 1)
+    out_mask = topo.mask(core, near[0])
+    in_mask = topo.mask(core, helpers[0][0]) & ~out_mask
+    sent = _send(g, T, topo, core, slot(own, PAY), [h for h, _d in helpers], [slot(0, PAY) for _h in helpers],
+                 in_mask, S.harr)
+    sent += _send(g, T, topo, core, slot(own, PAY), near, [slot(_pos(ranks, topo, d, core), PAY) for d in near],
+                  out_mask, S.arra)
+
+    n_arra = (na - 1) * _bits(out_mask)
+    n_arrb = nb * _bits(out_mask)
+
+    def weights(s, a, b, raw_a):
+        v.tensor_tensor(T.nn[:, raw_a:b], col(raw_a, b, CH), col(raw_a, b, CLO), AluOpType.add).then_inc(S["va%d" % s], 1)
+        v.wait_ge(S["va%d" % s], 1)
+        v.tensor_reduce(T.nn[:, b:b + 1], T.nn[:, a:b], AxisListType.X, AluOpType.min).then_inc(S["vm%d" % s], 1)
+        sc.wait_ge(S["vm%d" % s], 1)
+        sc.activation(T.f[:, a:b], T.nn[:, a:b], ActivationFunctionType.Exp, bias=T.nn[:, b:b + 1],
+                      scale=-1.0).then_inc(S["ex%d" % s], 1)
+        v.wait_ge(S["ex%d" % s], 1)
+
+    def products(order, ps, ncol, done):
+        for p in order:
+            v.tensor_scalar(T.dg[:, p * 128:(p + 1) * 128], T.ident[:], T.f[:, p:p + 1], None,
+                            AluOpType.mult).then_inc(S["d%d" % p], 1)
+        for k, p in enumerate(order):
+            pe.wait_ge(S["d%d" % p], 1)
+            if p == na:
+                pe.wait_ge(S.ev0, 1)
+            mm = pe.matmul(ps[:, 0:ncol], T.dg[:, p * 128:(p + 1) * 128], slot(p, ncol), k == 0, k == len(order) - 1)
+            if k == len(order) - 1:
+                mm.then_inc(done, 1)
+
+    v.wait_ge(S.pk2, 1)
+    v.wait_ge(S.pk3, 1)
+    v.wait_ge(S.idn, 1)
+    v.wait_ge(S.arra, n_arra)
+    pe.wait_ge(S.ldo, 16)
+    pe.wait_ge(S.arra, n_arra)
+    weights(0, 0, na, 0)
+    products(list(range(na)), T.psa, D + 1, S.pe0)
+    sc.wait_ge(S.pe0, 1)
+    sc.activation(slot(na, D + 1), T.psa[:, 0:D + 1], ActivationFunctionType.Copy).then_inc(S.ev0, 1)
+
+    a, b = na, NPOS
+    v.wait_ge(S.vm0, 1)
+    v.wait_ge(S.arrb, n_arrb)
+    pe.wait_ge(S.arrb, n_arrb)
+    weights(1, a, b, a + 1)
+    products(list(range(a + 1, b)) + [a], T.psb, D, S.pe1)
+    v.wait_ge(S.ev0, 1)
+    v.tensor_tensor(T.fl[:, 0:b - a], T.f[:, a:b], col(a, b, CL), AluOpType.mult).then_inc(S.fls, 1)
+    v.wait_ge(S.fls, 1)
+    v.tensor_reduce(T.den[:, 0:1], T.fl[:, 0:b - a], AxisListType.X, AluOpType.add).then_inc(S.dns, 1)
+    v.wait_ge(S.dns, 1)
+    v.reciprocal(T.rden[:, 0:1], T.den[:, 0:1]).then_inc(S.rcs, 1)
+    v.wait_ge(S.rcs, 1)
+    v.wait_ge(S.pe1, 1)
+    v.tensor_scalar(T.ysb[:], T.psb[:, 0:D], T.rden[:, 0:1], None, AluOpType.mult).then_inc(S.yv, 1)
+    sy.wait_ge(S.yv, 1)
+    sy.dma_start(T.y[:], T.ysb[:]).then_inc(S.st, 16)
+    sy.wait_ge(S.st, 16)
+    g.wait_ge(S.sent, sent)

@@ -3,18 +3,23 @@ from concourse.mybir import AluOpType, AxisListType, ActivationFunctionType
 
 W = 136
 D = 128
-CL, CH, CLO = 128, 129, 130
-PAY = 131
+C0 = 4
+CH, CQ, CL, CO = 5, 6, 7, 8
+PAY = W - C0
 NPOS = 10
+BIG = 100663296.0
+ENG = 8
 
 SCRATCH = {
     "land": ("sbuf", [128, NPOS * W], "bfloat16"),
-    "mlb": ("sbuf", [128, 2], "float32"),
+    "z": ("sbuf", [128, 20], "float32"),
     "ones": ("sbuf", [128, 128], "bfloat16"),
     "ident": ("sbuf", [128, 128], "bfloat16"),
     "dg": ("sbuf", [128, NPOS * 128], "bfloat16"),
-    "nn": ("sbuf", [128, 12], "float32"),
-    "f": ("sbuf", [128, 16], "bfloat16"),
+    "e1": ("sbuf", [128, 16], "bfloat16"),
+    "e2": ("sbuf", [128, 16], "bfloat16"),
+    "rb": ("sbuf", [128, 4], "float32"),
+    "ff": ("sbuf", [128, 12], "float32"),
     "fl": ("sbuf", [128, 12], "float32"),
     "den": ("sbuf", [128, 4], "float32"),
     "rden": ("sbuf", [128, 4], "float32"),
@@ -22,8 +27,8 @@ SCRATCH = {
     "psa": ("psum", [128, 512], "float32"),
     "psb": ("psum", [128, 512], "float32"),
 }
-SEMAPHORES = (["ldo", "ldm", "pk1", "pk2", "pk3", "one", "idn", "harr", "arra", "arrb", "sent", "st",
-               "va0", "va1", "vm0", "vm1", "ex0", "ex1", "pe0", "pe1", "ev0", "fls", "dns", "rcs", "yv"]
+SEMAPHORES = (["ldo", "ldm", "ms", "pk", "one", "idn", "harr", "arra", "arrb", "sent", "st",
+               "xo", "x2a", "x1a", "x2b", "x1b", "ra", "rbs", "pe0", "pe1", "ev0", "ffs", "fls", "dns", "rcs", "yv"]
               + ["d%d" % p for p in range(NPOS)])
 
 
@@ -31,8 +36,16 @@ def _bits(mask):
     return bin(mask).count("1")
 
 
+def _take(mask, k):
+    out, e = 0, 0
+    while _bits(out) < k:
+        out |= mask & (1 << e)
+        e += 1
+    return out
+
+
 def _groups(ranks, topo, r):
-    near = [x for x in ranks if x == r or topo.may_write(x, r)]
+    near = [r] + [x for x in ranks if x != r and topo.may_write(x, r)]
     far = [x for x in ranks if x not in near]
     return near, far
 
@@ -57,7 +70,11 @@ def _plan(ranks, topo, c):
     return near, [(h1, far[:k]), (h2, far[k:])]
 
 
-def _send(g, T, topo, src_core, src_ap, dests, dst_aps, mask, remote_sem):
+def _hand_mask(topo, r, h, off):
+    return _take(topo.mask(r, h) & ~topo.mask(r, off), ENG)
+
+
+def _send(g, T, topo, src_ap, dests, dst_aps, mask, remote_sem):
     ids = []
     for d in dests:
         rid, pid, _se = topo.addr(d)
@@ -71,7 +88,8 @@ def rank_program(g, core, T, topo):
     ranks = list(T.cores)
     land = T.land
     S = T.sem
-    slot = lambda p, n: land[:, p * W:p * W + n]
+    part = lambda p, c, n: land[:, p * W + c:p * W + c + n]
+    pay = lambda p: part(p, C0, PAY)
 
     if T.rank_of(core) is None:
         for r in ranks:
@@ -80,94 +98,108 @@ def rank_program(g, core, T, topo):
             for h, dests in _plan(ranks, topo, r)[1]:
                 if h != core:
                     continue
-                inside = topo.mask(r, h) & ~topo.mask(r, dests[0])
-                g.wait_ge(S.harr, _bits(inside))
-                n = _send(g, T, topo, core, slot(0, PAY), dests,
-                          [slot(_pos(ranks, topo, d, r), PAY) for d in dests], topo.mask(core, dests[0]), S.arrb)
+                g.wait_ge(S.harr, _bits(_hand_mask(topo, r, h, dests[0])))
+                n = _send(g, T, topo, pay(0), dests, [pay(_pos(ranks, topo, d, r)) for d in dests],
+                          _take(topo.mask(core, dests[0]), ENG), S.arrb)
                 g.wait_ge(S.sent, n)
         return
 
     v, sc, pe, sy = g.vector, g.scalar, g.tensor, g.sync
+    Exp = ActivationFunctionType.Exp
+    mult, add = AluOpType.mult, AluOpType.add
     near_in, far_in = _groups(ranks, topo, core)
     na, nb = len(near_in), len(far_in)
-    own = _pos(ranks, topo, core, core)
     near, helpers = _plan(ranks, topo, core)
     col = lambda a, b, k: land[:, a * W + k:(b - 1) * W + k + 1:W]
-    one = lambda p, k: land[:, p * W + k:p * W + k + 1]
+    dgp = lambda p: T.dg[:, p * 128:(p + 1) * 128]
+    a, b = na, NPOS
+    n_arra, n_arrb = (na - 1) * ENG, nb * ENG
 
-    sy.dma_start(slot(own, D), T.o[:]).then_inc(S.ldo, 16)
-    sc.dma_start(T.mlb[:], T.ml[:]).then_inc(S.ldm, 16)
+    sy.dma_start(part(0, CO, D), T.o[:]).then_inc(S.ldo, 16)
+    sc.dma_start(T.z[:, 4:6], T.ml[:]).then_inc(S.ldm, 16)
     v.memset(T.ones[:], 1.0).then_inc(S.one, 1)
+    v.memset(T.z[:, 2:3], BIG).then_inc(S.ms, 1)
+    v.memset(T.z[:, 3:4], -BIG).then_inc(S.ms, 1)
+    v.memset(T.z[:, 8:16], 1.0).then_inc(S.ms, 1)
+    v.memset(T.z[:, 16:20], 0.0).then_inc(S.ms, 1)
+    v.memset(part(a, CQ, 1), 0.0).then_inc(S.ms, 1)
     g.wait_ge(S.one, 1)
     g.affine_select(T.ident[:], T.ones[:], [[-1, 128]], AluOpType.is_equal, 0.0, 0, 1).then_inc(S.idn, 1)
 
+    v.wait_ge(S.ms, 5)
     v.wait_ge(S.ldm, 16)
-    v.tensor_scalar(one(own, CH), T.mlb[:, 0:1], -1.0, None, AluOpType.mult).then_inc(S.pk1, 1)
-    v.tensor_copy(one(own, CL), T.mlb[:, 1:2]).then_inc(S.pk3, 1)
-    v.wait_ge(S.pk1, 1)
-    v.tensor_scalar(one(own, CLO), T.mlb[:, 0:1], -1.0, one(own, CH), AluOpType.mult,
-                    AluOpType.subtract).then_inc(S.pk2, 1)
+    v.tensor_tensor_scan(part(0, C0, 4), T.z[:, 4:20:4], T.z[:, 2:6], -1.0, mult, add).then_inc(S.pk, 1)
 
     g.wait_ge(S.ldo, 16)
-    g.wait_ge(S.pk3, 1)
-    g.wait_ge(S.pk2, 1)
-    out_mask = topo.mask(core, near[0])
-    in_mask = topo.mask(core, helpers[0][0]) & ~out_mask
-    sent = _send(g, T, topo, core, slot(own, PAY), [h for h, _d in helpers], [slot(0, PAY) for _h in helpers],
-                 in_mask, S.harr)
-    sent += _send(g, T, topo, core, slot(own, PAY), near, [slot(_pos(ranks, topo, d, core), PAY) for d in near],
-                  out_mask, S.arra)
+    g.wait_ge(S.pk, 1)
+    sent = _send(g, T, topo, pay(0), [h for h, _d in helpers], [pay(0) for _h in helpers],
+                 _hand_mask(topo, core, helpers[0][0], near[0]), S.harr)
+    sent += _send(g, T, topo, pay(0), near, [pay(_pos(ranks, topo, d, core)) for d in near],
+                  _take(topo.mask(core, near[0]), ENG), S.arra)
 
-    n_arra = (na - 1) * _bits(out_mask)
-    n_arrb = nb * _bits(out_mask)
+    sc.wait_ge(S.pk, 1)
+    sc.activation(T.e2[:, 0:1], part(0, CQ, 1), Exp).then_inc(S.xo, 1)
+    sc.wait_ge(S.arra, n_arra)
+    sc.activation(T.e2[:, 1:na], col(1, na, CQ), Exp).then_inc(S.x2a, 1)
+    sc.wait_ge(S.ra, 1)
+    sc.activation(T.e1[:, 0:na], col(0, na, CH), Exp, bias=part(a, CH, 1), scale=-1.0).then_inc(S.x1a, 1)
+    sc.wait_ge(S.ms, 5)
+    sc.wait_ge(S.arrb, n_arrb)
+    sc.activation(T.e2[:, a:b], col(a, b, CQ), Exp).then_inc(S.x2b, 1)
+    sc.wait_ge(S.rbs, 1)
+    sc.activation(T.e1[:, a:b], col(a, b, CH), Exp, bias=T.rb[:, 0:1], scale=-1.0).then_inc(S.x1b, 1)
+    sc.wait_ge(S.pe0, 1)
+    sc.activation(part(a, CL, D + 1), T.psa[:, 0:D + 1], ActivationFunctionType.Copy).then_inc(S.ev0, 1)
 
-    def weights(s, a, b, raw_a):
-        v.tensor_tensor(T.nn[:, raw_a:b], col(raw_a, b, CH), col(raw_a, b, CLO), AluOpType.add).then_inc(S["va%d" % s], 1)
-        v.wait_ge(S["va%d" % s], 1)
-        v.tensor_reduce(T.nn[:, b:b + 1], T.nn[:, a:b], AxisListType.X, AluOpType.min).then_inc(S["vm%d" % s], 1)
-        sc.wait_ge(S["vm%d" % s], 1)
-        sc.activation(T.f[:, a:b], T.nn[:, a:b], ActivationFunctionType.Exp, bias=T.nn[:, b:b + 1],
-                      scale=-1.0).then_inc(S["ex%d" % s], 1)
-        v.wait_ge(S["ex%d" % s], 1)
+    def diag(p):
+        v.tensor_scalar(dgp(p), T.ident[:], T.e1[:, p:p + 1], T.e2[:, p:p + 1], mult, mult).then_inc(S["d%d" % p], 1)
 
-    def products(order, ps, ncol, done):
-        for p in order:
-            v.tensor_scalar(T.dg[:, p * 128:(p + 1) * 128], T.ident[:], T.f[:, p:p + 1], None,
-                            AluOpType.mult).then_inc(S["d%d" % p], 1)
+    def products(order, ps, c0, ncol, done):
         for k, p in enumerate(order):
             pe.wait_ge(S["d%d" % p], 1)
-            if p == na:
+            if p == a:
                 pe.wait_ge(S.ev0, 1)
-            mm = pe.matmul(ps[:, 0:ncol], T.dg[:, p * 128:(p + 1) * 128], slot(p, ncol), k == 0, k == len(order) - 1)
+            mm = pe.matmul(ps[:, 0:ncol], dgp(p), part(p, c0, ncol), k == 0, k == len(order) - 1)
             if k == len(order) - 1:
                 mm.then_inc(done, 1)
 
-    v.wait_ge(S.pk2, 1)
-    v.wait_ge(S.pk3, 1)
-    v.wait_ge(S.idn, 1)
+    v.wait_ge(S.pk, 1)
     v.wait_ge(S.arra, n_arra)
+    v.tensor_reduce(part(a, CH, 1), col(0, na, CH), AxisListType.X, AluOpType.min).then_inc(S.ra, 1)
+    v.wait_ge(S.idn, 1)
+    v.wait_ge(S.xo, 1)
+    v.wait_ge(S.x2a, 1)
+    v.wait_ge(S.x1a, 1)
+    for p in range(na):
+        diag(p)
     pe.wait_ge(S.ldo, 16)
     pe.wait_ge(S.arra, n_arra)
-    weights(0, 0, na, 0)
-    products(list(range(na)), T.psa, D + 1, S.pe0)
-    sc.wait_ge(S.pe0, 1)
-    sc.activation(slot(na, D + 1), T.psa[:, 0:D + 1], ActivationFunctionType.Copy).then_inc(S.ev0, 1)
+    products(list(range(na)), T.psa, CL, D + 1, S.pe0)
 
-    a, b = na, NPOS
-    v.wait_ge(S.vm0, 1)
+    order = list(range(a + 1, b)) + [a]
+    v.wait_ge(S.ra, 1)
     v.wait_ge(S.arrb, n_arrb)
+    v.tensor_reduce(T.rb[:, 0:1], col(a, b, CH), AxisListType.X, AluOpType.min).then_inc(S.rbs, 1)
+    v.wait_ge(S.x2b, 1)
+    v.wait_ge(S.x1b, 1)
+    for k, p in enumerate(order):
+        diag(p)
+        if k == 0:
+            v.tensor_tensor(T.ff[:, 0:b - a], T.e1[:, a:b], T.e2[:, a:b], mult).then_inc(S.ffs, 1)
+        if k == 2:
+            v.wait_ge(S.ffs, 1)
+            v.wait_ge(S.ev0, 1)
+            v.tensor_tensor(T.fl[:, 0:b - a], T.ff[:, 0:b - a], col(a, b, CL), mult).then_inc(S.fls, 1)
+        if k == 4:
+            v.wait_ge(S.fls, 1)
+            v.tensor_reduce(T.den[:, 0:1], T.fl[:, 0:b - a], AxisListType.X, add).then_inc(S.dns, 1)
     pe.wait_ge(S.arrb, n_arrb)
-    weights(1, a, b, a + 1)
-    products(list(range(a + 1, b)) + [a], T.psb, D, S.pe1)
-    v.wait_ge(S.ev0, 1)
-    v.tensor_tensor(T.fl[:, 0:b - a], T.f[:, a:b], col(a, b, CL), AluOpType.mult).then_inc(S.fls, 1)
-    v.wait_ge(S.fls, 1)
-    v.tensor_reduce(T.den[:, 0:1], T.fl[:, 0:b - a], AxisListType.X, AluOpType.add).then_inc(S.dns, 1)
+    products(order, T.psb, CO, D, S.pe1)
     v.wait_ge(S.dns, 1)
     v.reciprocal(T.rden[:, 0:1], T.den[:, 0:1]).then_inc(S.rcs, 1)
     v.wait_ge(S.rcs, 1)
     v.wait_ge(S.pe1, 1)
-    v.tensor_scalar(T.ysb[:], T.psb[:, 0:D], T.rden[:, 0:1], None, AluOpType.mult).then_inc(S.yv, 1)
+    v.tensor_scalar(T.ysb[:], T.psb[:, 0:D], T.rden[:, 0:1], None, mult).then_inc(S.yv, 1)
     sy.wait_ge(S.yv, 1)
     sy.dma_start(T.y[:], T.ysb[:]).then_inc(S.st, 16)
     sy.wait_ge(S.st, 16)

@@ -1,35 +1,37 @@
 from concourse.bass import DstId, RemoteDMATransfer
 from concourse.mybir import AluOpType, AxisListType, ActivationFunctionType
 
-W = 136
 D = 128
-C0 = 4
-CH, CQ, CL, CO = 5, 6, 7, 8
-PAY = W - C0
-NPOS = 10
+NR = 9
+MW = 4
 BIG = 100663296.0
 ENG = 8
+EM = 2
+EO = 16
 
 SCRATCH = {
-    "land": ("sbuf", [128, NPOS * W], "bfloat16"),
+    "land": ("sbuf", [128, NR * D], "bfloat16"),
+    "mls": ("sbuf", [128, NR * MW], "float32"),
+    "od": ("dram", [128, D], "bfloat16"),
+    "md": ("dram", [128, 2], "float32"),
     "z": ("sbuf", [128, 20], "float32"),
+    "hq": ("sbuf", [128, 4], "float32"),
+    "eo": ("sbuf", [128, 4], "float32"),
     "ones": ("sbuf", [128, 128], "bfloat16"),
     "ident": ("sbuf", [128, 128], "bfloat16"),
-    "dg": ("sbuf", [128, NPOS * 128], "bfloat16"),
-    "e1": ("sbuf", [128, 16], "bfloat16"),
-    "e2": ("sbuf", [128, 16], "bfloat16"),
-    "rb": ("sbuf", [128, 4], "float32"),
-    "ff": ("sbuf", [128, 12], "float32"),
+    "ido": ("sbuf", [128, 128], "bfloat16"),
+    "dg": ("sbuf", [128, NR * 128], "bfloat16"),
+    "nm": ("sbuf", [128, 4], "float32"),
+    "f": ("sbuf", [128, 12], "float32"),
     "fl": ("sbuf", [128, 12], "float32"),
     "den": ("sbuf", [128, 4], "float32"),
     "rden": ("sbuf", [128, 4], "float32"),
     "ysb": ("sbuf", [128, 128], "bfloat16"),
-    "psa": ("psum", [128, 512], "float32"),
-    "psb": ("psum", [128, 512], "float32"),
+    "ps": ("psum", [128, 512], "float32"),
 }
-SEMAPHORES = (["ldo", "ldm", "ms", "pk", "one", "idn", "harr", "arra", "arrb", "sent", "st",
-               "xo", "x2a", "x1a", "x2b", "x1b", "ra", "rbs", "pe0", "pe1", "ev0", "ffs", "fls", "dns", "rcs", "yv"]
-              + ["d%d" % p for p in range(NPOS)])
+SEMAPHORES = (["ldd", "ldmd", "ldo", "ldm", "ms", "pk", "one", "idn", "idr", "ids", "hm", "ho", "am", "sent", "st",
+               "xo", "own", "rm", "xf", "fls", "dns", "rcs", "pe1", "yv"]
+              + ["d%d" % p for p in range(NR)] + ["a%d" % p for p in range(NR)])
 
 
 def _bits(mask):
@@ -44,17 +46,6 @@ def _take(mask, k):
     return out
 
 
-def _groups(ranks, topo, r):
-    near = [r] + [x for x in ranks if x != r and topo.may_write(x, r)]
-    far = [x for x in ranks if x not in near]
-    return near, far
-
-
-def _pos(ranks, topo, r, s):
-    near, far = _groups(ranks, topo, r)
-    return near.index(s) if s in near else len(near) + 1 + far.index(s)
-
-
 def _plan(ranks, topo, c):
     i = ranks.index(c)
     n = len(ranks)
@@ -62,16 +53,26 @@ def _plan(ranks, topo, c):
     near = sorted([d for d in ranks if d != c and topo.may_write(c, d)], key=turn)
     far = sorted([d for d in ranks if d != c and not topo.may_write(c, d)],
                  key=lambda d: (topo.mates(topo.chip(c), topo.chip(d)), turn(d)))
-    cand = [x for x in range(topo.CORES_PER_CHIP * topo.CHIPS)
-            if topo.chip(x) == topo.chip(c) and x not in ranks and all(topo.may_write(x, d) for d in far)]
-    h1 = [x for x in cand if topo.die(x) == topo.die(c)][0]
-    h2 = [x for x in cand if topo.die(x) != topo.die(c)][0]
-    k = (len(far) + 1) // 2
-    return near, [(h1, far[:k]), (h2, far[k:])]
+    cores = [x for x in range(topo.CORES_PER_CHIP * topo.CHIPS) if topo.chip(x) == topo.chip(c) and x not in ranks]
+    mine = lambda x: topo.die(x) == topo.die(c)
+    able = [x for x in cores if all(topo.may_write(x, d) for d in far)]
+    port = [x for pair in zip([x for x in able if not mine(x)], [x for x in able if mine(x)]) for x in pair]
+    plain = sorted([x for x in cores if x not in able], key=mine)[::-1]
+    jobs = [(h, [d for k, d in enumerate(far) if k % len(port) == j]) for j, h in enumerate(port)]
+    direct, rest = near[:1], near[1:]
+    jobs += [(h, [d]) for h, d in zip(plain, rest)]
+    direct = direct + rest[len(plain):]
+    return direct, [(h, ds) for h, ds in jobs if ds]
 
 
-def _hand_mask(topo, r, h, off):
-    return _take(topo.mask(r, h) & ~topo.mask(r, off), ENG)
+def _slot(ranks, r, s):
+    return 0 if s == r else 1 + [x for x in ranks if x != r].index(s)
+
+
+def _share(k, n):
+    blocks = D // 8
+    lo, hi = (k * blocks) // n, ((k + 1) * blocks) // n
+    return lo * 8, (hi - lo) * 8
 
 
 def _send(g, T, topo, src_ap, dests, dst_aps, mask, remote_sem):
@@ -86,120 +87,106 @@ def _send(g, T, topo, src_ap, dests, dst_aps, mask, remote_sem):
 
 def rank_program(g, core, T, topo):
     ranks = list(T.cores)
-    land = T.land
     S = T.sem
-    part = lambda p, c, n: land[:, p * W + c:p * W + c + n]
-    pay = lambda p: part(p, C0, PAY)
+    slot_o = lambda p: T.land[:, p * D:(p + 1) * D]
+    slot_m = lambda p: T.mls[:, p * MW:p * MW + 2]
+    arr = lambda s: S["a%d" % ranks.index(s)]
 
     if T.rank_of(core) is None:
         for r in ranks:
             if topo.chip(r) != topo.chip(core):
                 continue
-            for h, dests in _plan(ranks, topo, r)[1]:
+            hs = _plan(ranks, topo, r)[1]
+            for k, (h, dests) in enumerate(hs):
                 if h != core:
                     continue
-                g.wait_ge(S.harr, _bits(_hand_mask(topo, r, h, dests[0])))
-                n = _send(g, T, topo, pay(0), dests, [pay(_pos(ranks, topo, d, r)) for d in dests],
-                          _take(topo.mask(core, dests[0]), ENG), S.arrb)
+                mask = _take(topo.mask(core, dests[0]) & topo.mask(core, r), ENG)
+                c0, wid = _share(k, len(hs))
+                idc = T.ident[:, c0:c0 + wid]
+                g.vector.memset(T.ones[:, 0:wid], 1.0).then_inc(S.one, 1)
+                g.wait_ge(S.one, 1)
+                g.affine_select(idc, T.ones[:, 0:wid], [[-1, wid]], AluOpType.is_equal, 0.0, -c0, 1).then_inc(S.idn, 1)
+                g.wait_ge(S.idn, 1)
+                n = _send(g, T, topo, idc, [r], [idc], mask, S.idr)
+                g.wait_ge(S.hm, EM)
+                n += _send(g, T, topo, T.md[:], dests, [slot_m(_slot(ranks, d, r)) for d in dests], mask, S.am)
+                g.wait_ge(S.ho, EO)
+                n += _send(g, T, topo, T.od[:], dests, [slot_o(_slot(ranks, d, r)) for d in dests], mask, arr(r))
                 g.wait_ge(S.sent, n)
         return
 
     v, sc, pe, sy = g.vector, g.scalar, g.tensor, g.sync
     Exp = ActivationFunctionType.Exp
     mult, add = AluOpType.mult, AluOpType.add
-    near_in, far_in = _groups(ranks, topo, core)
-    na, nb = len(near_in), len(far_in)
-    near, helpers = _plan(ranks, topo, core)
-    col = lambda a, b, k: land[:, a * W + k:(b - 1) * W + k + 1:W]
+    direct, helpers = _plan(ranks, topo, core)
+    hcores = [h for h, _d in helpers]
     dgp = lambda p: T.dg[:, p * 128:(p + 1) * 128]
-    a, b = na, NPOS
-    n_arra, n_arrb = (na - 1) * ENG, nb * ENG
+    m_all = T.mls[:, 0:NR * MW:MW]
+    l_all = T.mls[:, 1:NR * MW:MW]
+    n_am = (NR - 1) * ENG
 
-    sy.dma_start(part(0, CO, D), T.o[:]).then_inc(S.ldo, 16)
+    sy.dma_start(T.od[:], T.o[:]).then_inc(S.ldd, 16)
+    sc.dma_start(T.md[:], T.ml[:]).then_inc(S.ldmd, 16)
     sc.dma_start(T.z[:, 4:6], T.ml[:]).then_inc(S.ldm, 16)
-    v.memset(T.ones[:], 1.0).then_inc(S.one, 1)
+    sy.dma_start(slot_o(0), T.o[:]).then_inc(S.ldo, 16)
     v.memset(T.z[:, 2:3], BIG).then_inc(S.ms, 1)
     v.memset(T.z[:, 3:4], -BIG).then_inc(S.ms, 1)
-    v.memset(T.z[:, 8:16], 1.0).then_inc(S.ms, 1)
+    v.memset(T.z[:, 8:12], 1.0).then_inc(S.ms, 1)
+    v.memset(T.z[:, 12:16], -1.0).then_inc(S.ms, 1)
     v.memset(T.z[:, 16:20], 0.0).then_inc(S.ms, 1)
-    v.memset(part(a, CQ, 1), 0.0).then_inc(S.ms, 1)
-    g.wait_ge(S.one, 1)
-    g.affine_select(T.ident[:], T.ones[:], [[-1, 128]], AluOpType.is_equal, 0.0, 0, 1).then_inc(S.idn, 1)
+
+    g.wait_ge(S.ldmd, 16)
+    sent = _send(g, T, topo, T.md[:], hcores, [T.md[:] for _h in hcores], _take(topo.mask(core, hcores[0]), EM), S.hm)
+    g.wait_ge(S.ldd, 16)
+    sent += _send(g, T, topo, T.od[:], hcores, [T.od[:] for _h in hcores], _take(topo.mask(core, hcores[0]), EO), S.ho)
+    dmask = _take(topo.mask(core, direct[0]), ENG)
+    sent += _send(g, T, topo, T.md[:], direct, [slot_m(_slot(ranks, d, core)) for d in direct], dmask, S.am)
+    sent += _send(g, T, topo, T.od[:], direct, [slot_o(_slot(ranks, d, core)) for d in direct], dmask, arr(core))
 
     v.wait_ge(S.ms, 5)
     v.wait_ge(S.ldm, 16)
-    v.tensor_tensor_scan(part(0, C0, 4), T.z[:, 4:20:4], T.z[:, 2:6], -1.0, mult, add).then_inc(S.pk, 1)
-
-    g.wait_ge(S.ldo, 16)
-    g.wait_ge(S.pk, 1)
-    sent = _send(g, T, topo, pay(0), [h for h, _d in helpers], [pay(0) for _h in helpers],
-                 _hand_mask(topo, core, helpers[0][0], near[0]), S.harr)
-    sent += _send(g, T, topo, pay(0), near, [pay(_pos(ranks, topo, d, core)) for d in near],
-                  _take(topo.mask(core, near[0]), ENG), S.arra)
-
+    v.tensor_tensor_scan(T.hq[:, 0:4], T.z[:, 4:20:4], T.z[:, 2:6], 1.0, mult, add).then_inc(S.pk, 1)
     sc.wait_ge(S.pk, 1)
-    sc.activation(T.e2[:, 0:1], part(0, CQ, 1), Exp).then_inc(S.xo, 1)
-    sc.wait_ge(S.arra, n_arra)
-    sc.activation(T.e2[:, 1:na], col(1, na, CQ), Exp).then_inc(S.x2a, 1)
-    sc.wait_ge(S.ra, 1)
-    sc.activation(T.e1[:, 0:na], col(0, na, CH), Exp, bias=part(a, CH, 1), scale=-1.0).then_inc(S.x1a, 1)
-    sc.wait_ge(S.ms, 5)
-    sc.wait_ge(S.arrb, n_arrb)
-    sc.activation(T.e2[:, a:b], col(a, b, CQ), Exp).then_inc(S.x2b, 1)
-    sc.wait_ge(S.rbs, 1)
-    sc.activation(T.e1[:, a:b], col(a, b, CH), Exp, bias=T.rb[:, 0:1], scale=-1.0).then_inc(S.x1b, 1)
-    sc.wait_ge(S.pe0, 1)
-    sc.activation(part(a, CL, D + 1), T.psa[:, 0:D + 1], ActivationFunctionType.Copy).then_inc(S.ev0, 1)
-
-    def diag(p):
-        v.tensor_scalar(dgp(p), T.ident[:], T.e1[:, p:p + 1], T.e2[:, p:p + 1], mult, mult).then_inc(S["d%d" % p], 1)
-
-    def products(order, ps, c0, ncol, done):
-        for k, p in enumerate(order):
-            pe.wait_ge(S["d%d" % p], 1)
-            if p == a:
-                pe.wait_ge(S.ev0, 1)
-            mm = pe.matmul(ps[:, 0:ncol], dgp(p), part(p, c0, ncol), k == 0, k == len(order) - 1)
-            if k == len(order) - 1:
-                mm.then_inc(done, 1)
-
+    sc.activation(T.eo[:, 0:1], T.hq[:, 2:3], Exp).then_inc(S.xo, 1)
     v.wait_ge(S.pk, 1)
-    v.wait_ge(S.arra, n_arra)
-    v.tensor_reduce(part(a, CH, 1), col(0, na, CH), AxisListType.X, AluOpType.min).then_inc(S.ra, 1)
-    v.wait_ge(S.idn, 1)
+    v.tensor_copy(T.mls[:, 0:1], T.hq[:, 1:2]).then_inc(S.own, 1)
     v.wait_ge(S.xo, 1)
-    v.wait_ge(S.x2a, 1)
-    v.wait_ge(S.x1a, 1)
-    for p in range(na):
-        diag(p)
-    pe.wait_ge(S.ldo, 16)
-    pe.wait_ge(S.arra, n_arra)
-    products(list(range(na)), T.psa, CL, D + 1, S.pe0)
+    v.tensor_tensor(T.mls[:, 1:2], T.hq[:, 3:4], T.eo[:, 0:1], mult).then_inc(S.own, 1)
+    v.wait_ge(S.idr, ENG * len(helpers))
+    v.tensor_scalar(T.ido[:], T.ident[:], T.eo[:, 0:1], None, mult).then_inc(S.ids, 1)
 
-    order = list(range(a + 1, b)) + [a]
-    v.wait_ge(S.ra, 1)
-    v.wait_ge(S.arrb, n_arrb)
-    v.tensor_reduce(T.rb[:, 0:1], col(a, b, CH), AxisListType.X, AluOpType.min).then_inc(S.rbs, 1)
-    v.wait_ge(S.x2b, 1)
-    v.wait_ge(S.x1b, 1)
-    for k, p in enumerate(order):
-        diag(p)
-        if k == 0:
-            v.tensor_tensor(T.ff[:, 0:b - a], T.e1[:, a:b], T.e2[:, a:b], mult).then_inc(S.ffs, 1)
-        if k == 2:
-            v.wait_ge(S.ffs, 1)
-            v.wait_ge(S.ev0, 1)
-            v.tensor_tensor(T.fl[:, 0:b - a], T.ff[:, 0:b - a], col(a, b, CL), mult).then_inc(S.fls, 1)
-        if k == 4:
-            v.wait_ge(S.fls, 1)
-            v.tensor_reduce(T.den[:, 0:1], T.fl[:, 0:b - a], AxisListType.X, add).then_inc(S.dns, 1)
-    pe.wait_ge(S.arrb, n_arrb)
-    products(order, T.psb, CO, D, S.pe1)
+    v.wait_ge(S.own, 2)
+    v.wait_ge(S.am, n_am)
+    v.tensor_reduce(T.nm[:, 0:1], m_all, AxisListType.X, AluOpType.max, negate=True).then_inc(S.rm, 1)
+    sc.wait_ge(S.own, 2)
+    sc.wait_ge(S.am, n_am)
+    sc.wait_ge(S.rm, 1)
+    sc.activation(T.f[:, 0:NR], m_all, Exp, bias=T.nm[:, 0:1]).then_inc(S.xf, 1)
+    v.wait_ge(S.xf, 1)
+    v.tensor_tensor(T.fl[:, 0:NR], T.f[:, 0:NR], l_all, mult).then_inc(S.fls, 1)
+    v.wait_ge(S.fls, 1)
+    v.tensor_reduce(T.den[:, 0:1], T.fl[:, 0:NR], AxisListType.X, add).then_inc(S.dns, 1)
     v.wait_ge(S.dns, 1)
     v.reciprocal(T.rden[:, 0:1], T.den[:, 0:1]).then_inc(S.rcs, 1)
     v.wait_ge(S.rcs, 1)
+    v.wait_ge(S.ids, 1)
+
+    first = [s for s in ranks if s != core and core in _plan(ranks, topo, s)[0]]
+    order = [core] + first + [s for s in ranks if s != core and s not in first]
+    for k, s in enumerate(order):
+        p = _slot(ranks, core, s)
+        v.tensor_scalar(dgp(p), T.ido[:] if s == core else T.ident[:], T.f[:, p:p + 1], T.rden[:, 0:1],
+                        mult, mult).then_inc(S["d%d" % p], 1)
+        pe.wait_ge(S["d%d" % p], 1)
+        if s == core:
+            pe.wait_ge(S.ldo, 16)
+        else:
+            pe.wait_ge(arr(s), ENG)
+        mm = pe.matmul(T.ps[:, 0:D], dgp(p), slot_o(p), k == 0, k == len(order) - 1)
+        if k == len(order) - 1:
+            mm.then_inc(S.pe1, 1)
     v.wait_ge(S.pe1, 1)
-    v.tensor_scalar(T.ysb[:], T.psb[:, 0:D], T.rden[:, 0:1], None, mult).then_inc(S.yv, 1)
+    v.tensor_copy(T.ysb[:], T.ps[:, 0:D]).then_inc(S.yv, 1)
     sy.wait_ge(S.yv, 1)
     sy.dma_start(T.y[:], T.ysb[:]).then_inc(S.st, 16)
     sy.wait_ge(S.st, 16)

@@ -69,6 +69,13 @@ def _slot(ranks, r, s):
     return 0 if s == r else 1 + [x for x in ranks if x != r].index(s)
 
 
+def _when(ranks, topo, s, r):
+    direct, helpers = _plan(ranks, topo, s)
+    if r in direct:
+        return (0, len(helpers))
+    return [(ds.index(r), k) for k, (_h, ds) in enumerate(helpers) if r in ds][0]
+
+
 def _share(k, n):
     blocks = D // 8
     lo, hi = (k * blocks) // n, ((k + 1) * blocks) // n
@@ -109,7 +116,8 @@ def rank_program(g, core, T, topo):
                 g.wait_ge(S.idn, 1)
                 n = _send(g, T, topo, idc, [r], [idc], mask, S.idr)
                 g.wait_ge(S.hm, EM)
-                n += _send(g, T, topo, T.md[:], dests, [slot_m(_slot(ranks, d, r)) for d in dests], mask, S.am)
+                mld = dests + (_plan(ranks, topo, r)[0] if k == len(hs) - 1 else [])
+                n += _send(g, T, topo, T.md[:], mld, [slot_m(_slot(ranks, d, r)) for d in mld], mask, S.am)
                 g.wait_ge(S.ho, EO)
                 n += _send(g, T, topo, T.od[:], dests, [slot_o(_slot(ranks, d, r)) for d in dests], mask, arr(r))
                 g.wait_ge(S.sent, n)
@@ -138,9 +146,10 @@ def rank_program(g, core, T, topo):
     g.wait_ge(S.ldmd, 16)
     sent = _send(g, T, topo, T.md[:], hcores, [T.md[:] for _h in hcores], _take(topo.mask(core, hcores[0]), EM), S.hm)
     g.wait_ge(S.ldd, 16)
-    sent += _send(g, T, topo, T.od[:], hcores, [T.od[:] for _h in hcores], _take(topo.mask(core, hcores[0]), EO), S.ho)
+    for group in ([h for h, ds in helpers if not topo.may_write(core, ds[0])],
+                  [h for h, ds in helpers if topo.may_write(core, ds[0])]):
+        sent += _send(g, T, topo, T.od[:], group, [T.od[:] for _h in group], _take(topo.mask(core, group[0]), EO), S.ho)
     dmask = _take(topo.mask(core, direct[0]), ENG)
-    sent += _send(g, T, topo, T.md[:], direct, [slot_m(_slot(ranks, d, core)) for d in direct], dmask, S.am)
     sent += _send(g, T, topo, T.od[:], direct, [slot_o(_slot(ranks, d, core)) for d in direct], dmask, arr(core))
 
     v.wait_ge(S.ms, 5)
@@ -163,20 +172,21 @@ def rank_program(g, core, T, topo):
     sc.wait_ge(S.rm, 1)
     sc.activation(T.f[:, 0:NR], m_all, Exp, bias=T.nm[:, 0:1]).then_inc(S.xf, 1)
     v.wait_ge(S.xf, 1)
-    v.tensor_tensor(T.fl[:, 0:NR], T.f[:, 0:NR], l_all, mult).then_inc(S.fls, 1)
-    v.wait_ge(S.fls, 1)
-    v.tensor_reduce(T.den[:, 0:1], T.fl[:, 0:NR], AxisListType.X, add).then_inc(S.dns, 1)
-    v.wait_ge(S.dns, 1)
-    v.reciprocal(T.rden[:, 0:1], T.den[:, 0:1]).then_inc(S.rcs, 1)
-    v.wait_ge(S.rcs, 1)
     v.wait_ge(S.ids, 1)
 
-    first = [s for s in ranks if s != core and core in _plan(ranks, topo, s)[0]]
-    order = [core] + first + [s for s in ranks if s != core and s not in first]
+    order = [core] + sorted([s for s in ranks if s != core], key=lambda s: _when(ranks, topo, s, core))
     for k, s in enumerate(order):
         p = _slot(ranks, core, s)
-        v.tensor_scalar(dgp(p), T.ido[:] if s == core else T.ident[:], T.f[:, p:p + 1], T.rden[:, 0:1],
-                        mult, mult).then_inc(S["d%d" % p], 1)
+        v.tensor_scalar(dgp(p), T.ido[:] if s == core else T.ident[:], T.f[:, p:p + 1], None,
+                        mult).then_inc(S["d%d" % p], 1)
+        if k == 1:
+            v.tensor_tensor(T.fl[:, 0:NR], T.f[:, 0:NR], l_all, mult).then_inc(S.fls, 1)
+        if k == 3:
+            v.wait_ge(S.fls, 1)
+            v.tensor_reduce(T.den[:, 0:1], T.fl[:, 0:NR], AxisListType.X, add).then_inc(S.dns, 1)
+        if k == 6:
+            v.wait_ge(S.dns, 1)
+            v.reciprocal(T.rden[:, 0:1], T.den[:, 0:1]).then_inc(S.rcs, 1)
         pe.wait_ge(S["d%d" % p], 1)
         if s == core:
             pe.wait_ge(S.ldo, 16)
@@ -185,8 +195,9 @@ def rank_program(g, core, T, topo):
         mm = pe.matmul(T.ps[:, 0:D], dgp(p), slot_o(p), k == 0, k == len(order) - 1)
         if k == len(order) - 1:
             mm.then_inc(S.pe1, 1)
+    v.wait_ge(S.rcs, 1)
     v.wait_ge(S.pe1, 1)
-    v.tensor_copy(T.ysb[:], T.ps[:, 0:D]).then_inc(S.yv, 1)
+    v.tensor_scalar(T.ysb[:], T.ps[:, 0:D], T.rden[:, 0:1], None, mult).then_inc(S.yv, 1)
     sy.wait_ge(S.yv, 1)
     sy.dma_start(T.y[:], T.ysb[:]).then_inc(S.st, 16)
     sy.wait_ge(S.st, 16)

@@ -7,7 +7,7 @@ MW = 4
 BIG = 100663296.0
 ENG = 8
 EM = 2
-EO = 16
+EO = 8
 
 SCRATCH = {
     "land": ("sbuf", [128, NR * D], "bfloat16"),
@@ -18,18 +18,19 @@ SCRATCH = {
     "hq": ("sbuf", [128, 4], "float32"),
     "eo": ("sbuf", [128, 4], "float32"),
     "ones": ("sbuf", [128, 128], "bfloat16"),
+    "idx": ("sbuf", [128, 128], "bfloat16"),
     "ident": ("sbuf", [128, 128], "bfloat16"),
     "ido": ("sbuf", [128, 128], "bfloat16"),
     "dg": ("sbuf", [128, NR * 128], "bfloat16"),
     "nm": ("sbuf", [128, 4], "float32"),
-    "f": ("sbuf", [128, 12], "float32"),
+    "f": ("sbuf", [128, 16], "bfloat16"),
     "fl": ("sbuf", [128, 12], "float32"),
     "den": ("sbuf", [128, 4], "float32"),
     "rden": ("sbuf", [128, 4], "float32"),
     "ysb": ("sbuf", [128, 128], "bfloat16"),
     "ps": ("psum", [128, 512], "float32"),
 }
-SEMAPHORES = (["ldd", "ldmd", "ldo", "ldm", "ms", "pk", "one", "idn", "idr", "ids", "hm", "ho", "am", "sent", "st",
+SEMAPHORES = (["ldd", "ldmd", "ldo", "ldm", "ms", "pk", "one", "idn", "idr", "ids", "hm", "ho", "am", "sent", "st", "go",
                "xo", "own", "rm", "xf", "fls", "dns", "rcs", "pe1", "yv"]
               + ["d%d" % p for p in range(NR)] + ["a%d" % p for p in range(NR)])
 
@@ -44,6 +45,10 @@ def _take(mask, k):
         out |= mask & (1 << e)
         e += 1
     return out
+
+
+def _nth(mask, k):
+    return _take(mask, k + 1) & ~_take(mask, k) if k else _take(mask, 1)
 
 
 def _plan(ranks, topo, c):
@@ -65,6 +70,11 @@ def _plan(ranks, topo, c):
     return direct, [(h, ds) for h, ds in jobs if ds]
 
 
+def _ml_dests(ranks, topo, r):
+    direct, hs = _plan(ranks, topo, r)
+    return [ds + (direct if k == len(hs) - 1 else []) for k, (_h, ds) in enumerate(hs)]
+
+
 def _slot(ranks, r, s):
     return 0 if s == r else 1 + [x for x in ranks if x != r].index(s)
 
@@ -72,7 +82,7 @@ def _slot(ranks, r, s):
 def _when(ranks, topo, s, r):
     direct, helpers = _plan(ranks, topo, s)
     if r in direct:
-        return (0, len(helpers))
+        return (-1, 0)
     return [(ds.index(r), k) for k, (_h, ds) in enumerate(helpers) if r in ds][0]
 
 
@@ -82,14 +92,24 @@ def _share(k, n):
     return lo * 8, (hi - lo) * 8
 
 
+def _id(topo, d):
+    rid, pid, _se = topo.addr(d)
+    return DstId(rid=rid, pnc=pid)
+
+
 def _send(g, T, topo, src_ap, dests, dst_aps, mask, remote_sem):
-    ids = []
-    for d in dests:
-        rid, pid, _se = topo.addr(d)
-        ids.append(DstId(rid=rid, pnc=pid))
-    g.remote_dma_fused([RemoteDMATransfer(dst_ids=ids, dma_engine_mask=mask, remote_sem=remote_sem,
-                                          srcs=[src_ap], dsts=dst_aps, alu_op=0)], local_sem=T.sem.sent)
+    g.remote_dma_fused([RemoteDMATransfer(dst_ids=[_id(topo, d) for d in dests], dma_engine_mask=mask,
+                                          remote_sem=remote_sem, srcs=[src_ap], dsts=dst_aps, alu_op=0)],
+                       local_sem=T.sem.sent)
     return _bits(mask)
+
+
+def _make_share(g, T, buf, c0, wid):
+    S = T.sem
+    g.vector.memset(T.ones[:, 0:wid], 1.0).then_inc(S.one, 1)
+    g.wait_ge(S.one, 1)
+    g.affine_select(buf, T.ones[:, 0:wid], [[-1, wid]], AluOpType.is_equal, 0.0, -c0, 1).then_inc(S.idn, 1)
+    g.wait_ge(S.idn, 1)
 
 
 def rank_program(g, core, T, topo):
@@ -108,15 +128,12 @@ def rank_program(g, core, T, topo):
                 if h != core:
                     continue
                 mask = _take(topo.mask(core, dests[0]) & topo.mask(core, r), ENG)
-                c0, wid = _share(k, len(hs))
+                c0, wid = _share(k, len(hs) + 1)
                 idc = T.ident[:, c0:c0 + wid]
-                g.vector.memset(T.ones[:, 0:wid], 1.0).then_inc(S.one, 1)
-                g.wait_ge(S.one, 1)
-                g.affine_select(idc, T.ones[:, 0:wid], [[-1, wid]], AluOpType.is_equal, 0.0, -c0, 1).then_inc(S.idn, 1)
-                g.wait_ge(S.idn, 1)
+                _make_share(g, T, idc, c0, wid)
                 n = _send(g, T, topo, idc, [r], [idc], mask, S.idr)
-                g.wait_ge(S.hm, EM)
-                mld = dests + (_plan(ranks, topo, r)[0] if k == len(hs) - 1 else [])
+                g.wait_ge(S.hm, 1)
+                mld = _ml_dests(ranks, topo, r)[k]
                 n += _send(g, T, topo, T.md[:], mld, [slot_m(_slot(ranks, d, r)) for d in mld], mask, S.am)
                 g.wait_ge(S.ho, EO)
                 n += _send(g, T, topo, T.od[:], dests, [slot_o(_slot(ranks, d, r)) for d in dests], mask, arr(r))
@@ -132,24 +149,41 @@ def rank_program(g, core, T, topo):
     m_all = T.mls[:, 0:NR * MW:MW]
     l_all = T.mls[:, 1:NR * MW:MW]
     n_am = (NR - 1) * ENG
+    out_eng = topo.mask(core, direct[0])
+    in_eng = topo.mask(core, hcores[0]) & ~out_eng
+    dmask = _take(out_eng, ENG)
 
     sy.dma_start(T.od[:], T.o[:]).then_inc(S.ldd, 16)
     sc.dma_start(T.md[:], T.ml[:]).then_inc(S.ldmd, 16)
     sc.dma_start(T.z[:, 4:6], T.ml[:]).then_inc(S.ldm, 16)
-    sy.dma_start(slot_o(0), T.o[:]).then_inc(S.ldo, 16)
+
+    nxt = direct[0]
+    nh = len(_plan(ranks, topo, nxt)[1])
+    c0, wid = _share(nh, nh + 1)
+    _make_share(g, T, T.idx[:, 0:wid], c0, wid)
+    sent = _send(g, T, topo, T.idx[:, 0:wid], [nxt], [T.ident[:, c0:c0 + wid]], dmask, S.idr)
+
     v.memset(T.z[:, 2:3], BIG).then_inc(S.ms, 1)
     v.memset(T.z[:, 3:4], -BIG).then_inc(S.ms, 1)
     v.memset(T.z[:, 8:12], 1.0).then_inc(S.ms, 1)
     v.memset(T.z[:, 12:16], -1.0).then_inc(S.ms, 1)
     v.memset(T.z[:, 16:20], 0.0).then_inc(S.ms, 1)
 
+    mlds = _ml_dests(ranks, topo, core)
+    first = sorted(range(len(hcores)), key=lambda k: (-len(mlds[k]), k))
     g.wait_ge(S.ldmd, 16)
-    sent = _send(g, T, topo, T.md[:], hcores, [T.md[:] for _h in hcores], _take(topo.mask(core, hcores[0]), EM), S.hm)
+    g.remote_dma_fused([RemoteDMATransfer(dst_ids=[_id(topo, hcores[k]) for k in first[e::EM]],
+                                          dma_engine_mask=_nth(in_eng, e), remote_sem=S.hm, srcs=[T.md[:]],
+                                          dsts=[T.md[:] for _k in first[e::EM]], alu_op=0)
+                        for e in range(EM)], local_sem=S.sent)
+    sent += EM
+    g.sem_inc(S.go, 1)
+    sy.wait_ge(S.go, 1)
+    sy.dma_start(slot_o(0), T.o[:]).then_inc(S.ldo, 16)
     g.wait_ge(S.ldd, 16)
     for group in ([h for h, ds in helpers if not topo.may_write(core, ds[0])],
                   [h for h, ds in helpers if topo.may_write(core, ds[0])]):
-        sent += _send(g, T, topo, T.od[:], group, [T.od[:] for _h in group], _take(topo.mask(core, group[0]), EO), S.ho)
-    dmask = _take(topo.mask(core, direct[0]), ENG)
+        sent += _send(g, T, topo, T.od[:], group, [T.od[:] for _h in group], _take(in_eng, EO), S.ho)
     sent += _send(g, T, topo, T.od[:], direct, [slot_o(_slot(ranks, d, core)) for d in direct], dmask, arr(core))
 
     v.wait_ge(S.ms, 5)
@@ -161,7 +195,7 @@ def rank_program(g, core, T, topo):
     v.tensor_copy(T.mls[:, 0:1], T.hq[:, 1:2]).then_inc(S.own, 1)
     v.wait_ge(S.xo, 1)
     v.tensor_tensor(T.mls[:, 1:2], T.hq[:, 3:4], T.eo[:, 0:1], mult).then_inc(S.own, 1)
-    v.wait_ge(S.idr, ENG * len(helpers))
+    v.wait_ge(S.idr, ENG * (len(helpers) + 1))
     v.tensor_scalar(T.ido[:], T.ident[:], T.eo[:, 0:1], None, mult).then_inc(S.ids, 1)
 
     v.wait_ge(S.own, 2)
@@ -175,16 +209,17 @@ def rank_program(g, core, T, topo):
     v.wait_ge(S.ids, 1)
 
     order = [core] + sorted([s for s in ranks if s != core], key=lambda s: _when(ranks, topo, s, core))
+    last = len(order) - 1
     for k, s in enumerate(order):
         p = _slot(ranks, core, s)
         v.tensor_scalar(dgp(p), T.ido[:] if s == core else T.ident[:], T.f[:, p:p + 1], None,
                         mult).then_inc(S["d%d" % p], 1)
-        if k == 1:
+        if k == 2:
             v.tensor_tensor(T.fl[:, 0:NR], T.f[:, 0:NR], l_all, mult).then_inc(S.fls, 1)
-        if k == 3:
+        if k == 4:
             v.wait_ge(S.fls, 1)
             v.tensor_reduce(T.den[:, 0:1], T.fl[:, 0:NR], AxisListType.X, add).then_inc(S.dns, 1)
-        if k == 6:
+        if k == last:
             v.wait_ge(S.dns, 1)
             v.reciprocal(T.rden[:, 0:1], T.den[:, 0:1]).then_inc(S.rcs, 1)
         pe.wait_ge(S["d%d" % p], 1)
@@ -192,8 +227,8 @@ def rank_program(g, core, T, topo):
             pe.wait_ge(S.ldo, 16)
         else:
             pe.wait_ge(arr(s), ENG)
-        mm = pe.matmul(T.ps[:, 0:D], dgp(p), slot_o(p), k == 0, k == len(order) - 1)
-        if k == len(order) - 1:
+        mm = pe.matmul(T.ps[:, 0:D], dgp(p), slot_o(p), k == 0, k == last)
+        if k == last:
             mm.then_inc(S.pe1, 1)
     v.wait_ge(S.rcs, 1)
     v.wait_ge(S.pe1, 1)

@@ -17,8 +17,8 @@ SCRATCH = {
     "z": ("sbuf", [128, 20], "float32"),
     "hq": ("sbuf", [128, 4], "float32"),
     "eo": ("sbuf", [128, 4], "float32"),
-    "ones": ("sbuf", [128, 128], "bfloat16"),
     "idx": ("sbuf", [128, 128], "bfloat16"),
+    "dif": ("sbuf", [128, 128], "bfloat16"),
     "ident": ("sbuf", [128, 128], "bfloat16"),
     "ido": ("sbuf", [128, 128], "bfloat16"),
     "dg": ("sbuf", [128, NR * 128], "bfloat16"),
@@ -30,7 +30,7 @@ SCRATCH = {
     "ysb": ("sbuf", [128, 128], "bfloat16"),
     "ps": ("psum", [128, 512], "float32"),
 }
-SEMAPHORES = (["ldd", "ldmd", "ldo", "ldm", "ms", "pk", "one", "idn", "idr", "ids", "hm", "ho", "am", "sent", "st", "go",
+SEMAPHORES = (["ldd", "ldmd", "ldo", "ldm", "ms", "pk", "idn", "idr", "ids", "hm", "ho", "am", "sent", "st", "go",
                "xo", "own", "rm", "xf", "fls", "dns", "rcs", "pe1", "yv"]
               + ["d%d" % p for p in range(NR)] + ["a%d" % p for p in range(NR)])
 
@@ -106,9 +106,7 @@ def _send(g, T, topo, src_ap, dests, dst_aps, mask, remote_sem):
 
 def _make_share(g, T, buf, c0, wid):
     S = T.sem
-    g.vector.memset(T.ones[:, 0:wid], 1.0).then_inc(S.one, 1)
-    g.wait_ge(S.one, 1)
-    g.affine_select(buf, T.ones[:, 0:wid], [[-1, wid]], AluOpType.is_equal, 0.0, -c0, 1).then_inc(S.idn, 1)
+    g.iota(buf, [[-1, wid]], -c0, 1, allow_small_or_imprecise_dtypes=True).then_inc(S.idn, 1)
     g.wait_ge(S.idn, 1)
 
 
@@ -129,7 +127,7 @@ def rank_program(g, core, T, topo):
                     continue
                 mask = _take(topo.mask(core, dests[0]) & topo.mask(core, r), ENG)
                 c0, wid = _share(k, len(hs) + 1)
-                idc = T.ident[:, c0:c0 + wid]
+                idc = T.dif[:, c0:c0 + wid]
                 _make_share(g, T, idc, c0, wid)
                 n = _send(g, T, topo, idc, [r], [idc], mask, S.idr)
                 g.wait_ge(S.hm, 1)
@@ -161,7 +159,7 @@ def rank_program(g, core, T, topo):
     nh = len(_plan(ranks, topo, nxt)[1])
     c0, wid = _share(nh, nh + 1)
     _make_share(g, T, T.idx[:, 0:wid], c0, wid)
-    sent = _send(g, T, topo, T.idx[:, 0:wid], [nxt], [T.ident[:, c0:c0 + wid]], dmask, S.idr)
+    sent = _send(g, T, topo, T.idx[:, 0:wid], [nxt], [T.dif[:, c0:c0 + wid]], dmask, S.idr)
 
     v.memset(T.z[:, 2:3], BIG).then_inc(S.ms, 1)
     v.memset(T.z[:, 3:4], -BIG).then_inc(S.ms, 1)
@@ -196,7 +194,8 @@ def rank_program(g, core, T, topo):
     v.wait_ge(S.xo, 1)
     v.tensor_tensor(T.mls[:, 1:2], T.hq[:, 3:4], T.eo[:, 0:1], mult).then_inc(S.own, 1)
     v.wait_ge(S.idr, ENG * (len(helpers) + 1))
-    v.tensor_scalar(T.ido[:], T.ident[:], T.eo[:, 0:1], None, mult).then_inc(S.ids, 1)
+    v.tensor_scalar(T.ident[:], T.dif[:], 0.0, None, AluOpType.is_equal).then_inc(S.ids, 1)
+    v.tensor_scalar(T.ido[:], T.dif[:], 0.0, T.eo[:, 0:1], AluOpType.is_equal, mult).then_inc(S.ids, 1)
 
     v.wait_ge(S.own, 2)
     v.wait_ge(S.am, n_am)
@@ -206,7 +205,7 @@ def rank_program(g, core, T, topo):
     sc.wait_ge(S.rm, 1)
     sc.activation(T.f[:, 0:NR], m_all, Exp, bias=T.nm[:, 0:1]).then_inc(S.xf, 1)
     v.wait_ge(S.xf, 1)
-    v.wait_ge(S.ids, 1)
+    v.wait_ge(S.ids, 2)
 
     order = [core] + sorted([s for s in ranks if s != core], key=lambda s: _when(ranks, topo, s, core))
     last = len(order) - 1

from concourse.bass import DstId, RemoteDMATransfer
from concourse.mybir import AluOpType, AxisListType, ActivationFunctionType

D = 128
NR = 9
MW = 4
BIG = 100663296.0
ENG = 8
EM = 2
EO = 8

SCRATCH = {
    "land": ("sbuf", [128, NR * D], "bfloat16"),
    "mls": ("sbuf", [128, NR * MW], "float32"),
    "od": ("dram", [128, D], "bfloat16"),
    "md": ("dram", [128, 2], "float32"),
    "z": ("sbuf", [128, 20], "float32"),
    "hq": ("sbuf", [128, 4], "float32"),
    "eo": ("sbuf", [128, 4], "float32"),
    "idx": ("sbuf", [128, 128], "bfloat16"),
    "dif": ("sbuf", [128, 128], "bfloat16"),
    "ident": ("sbuf", [128, 128], "bfloat16"),
    "ido": ("sbuf", [128, 128], "bfloat16"),
    "dg": ("sbuf", [128, NR * 128], "bfloat16"),
    "nm": ("sbuf", [128, 4], "float32"),
    "f": ("sbuf", [128, 16], "bfloat16"),
    "fl": ("sbuf", [128, 12], "float32"),
    "den": ("sbuf", [128, 4], "float32"),
    "rden": ("sbuf", [128, 4], "float32"),
    "ysb": ("sbuf", [128, 128], "bfloat16"),
    "ps": ("psum", [128, 512], "float32"),
}
SEMAPHORES = (["ldd", "ldmd", "ldo", "ldm", "ms", "pk", "idn", "idr", "ids", "hm", "ho", "am", "sent", "st", "go",
               "xo", "own", "rm", "xf", "fls", "dns", "rcs", "pe1", "yv"]
              + ["d%d" % p for p in range(NR)] + ["a%d" % p for p in range(NR)])


def _bits(mask):
    return bin(mask).count("1")


def _take(mask, k):
    out, e = 0, 0
    while _bits(out) < k:
        out |= mask & (1 << e)
        e += 1
    return out


def _nth(mask, k):
    return _take(mask, k + 1) & ~_take(mask, k) if k else _take(mask, 1)


def _plan(ranks, topo, c):
    i = ranks.index(c)
    n = len(ranks)
    turn = lambda d: (ranks.index(d) - i) % n
    near = sorted([d for d in ranks if d != c and topo.may_write(c, d)], key=turn)
    far = sorted([d for d in ranks if d != c and not topo.may_write(c, d)],
                 key=lambda d: (topo.mates(topo.chip(c), topo.chip(d)), turn(d)))
    cores = [x for x in range(topo.CORES_PER_CHIP * topo.CHIPS) if topo.chip(x) == topo.chip(c) and x not in ranks]
    mine = lambda x: topo.die(x) == topo.die(c)
    able = [x for x in cores if all(topo.may_write(x, d) for d in far)]
    port = [x for pair in zip([x for x in able if not mine(x)], [x for x in able if mine(x)]) for x in pair]
    plain = sorted([x for x in cores if x not in able], key=mine)[::-1]
    jobs = [(h, [d for k, d in enumerate(far) if k % len(port) == j]) for j, h in enumerate(port)]
    direct, rest = near[:1], near[1:]
    jobs += [(h, [d]) for h, d in zip(plain, rest)]
    direct = direct + rest[len(plain):]
    return direct, [(h, ds) for h, ds in jobs if ds]


def _ml_dests(ranks, topo, r):
    direct, hs = _plan(ranks, topo, r)
    return [ds + (direct if k == len(hs) - 1 else []) for k, (_h, ds) in enumerate(hs)]


def _slot(ranks, r, s):
    return 0 if s == r else 1 + [x for x in ranks if x != r].index(s)


def _when(ranks, topo, s, r):
    direct, helpers = _plan(ranks, topo, s)
    if r in direct:
        return (-1, 0)
    return [(ds.index(r), k) for k, (_h, ds) in enumerate(helpers) if r in ds][0]


def _share(k, n):
    blocks = D // 8
    lo, hi = (k * blocks) // n, ((k + 1) * blocks) // n
    return lo * 8, (hi - lo) * 8


def _id(topo, d):
    rid, pid, _se = topo.addr(d)
    return DstId(rid=rid, pnc=pid)


def _send(g, T, topo, src_ap, dests, dst_aps, mask, remote_sem):
    g.remote_dma_fused([RemoteDMATransfer(dst_ids=[_id(topo, d) for d in dests], dma_engine_mask=mask,
                                          remote_sem=remote_sem, srcs=[src_ap], dsts=dst_aps, alu_op=0)],
                       local_sem=T.sem.sent)
    return _bits(mask)


def _make_share(g, T, buf, c0, wid):
    S = T.sem
    g.iota(buf, [[-1, wid]], -c0, 1, allow_small_or_imprecise_dtypes=True).then_inc(S.idn, 1)
    g.wait_ge(S.idn, 1)


def rank_program(g, core, T, topo):
    ranks = list(T.cores)
    S = T.sem
    slot_o = lambda p: T.land[:, p * D:(p + 1) * D]
    slot_m = lambda p: T.mls[:, p * MW:p * MW + 2]
    arr = lambda s: S["a%d" % ranks.index(s)]

    if T.rank_of(core) is None:
        for r in ranks:
            if topo.chip(r) != topo.chip(core):
                continue
            hs = _plan(ranks, topo, r)[1]
            for k, (h, dests) in enumerate(hs):
                if h != core:
                    continue
                mask = _take(topo.mask(core, dests[0]) & topo.mask(core, r), ENG)
                c0, wid = _share(k, len(hs) + 1)
                idc = T.dif[:, c0:c0 + wid]
                _make_share(g, T, idc, c0, wid)
                n = _send(g, T, topo, idc, [r], [idc], mask, S.idr)
                g.wait_ge(S.hm, 1)
                mld = _ml_dests(ranks, topo, r)[k]
                n += _send(g, T, topo, T.md[:], mld, [slot_m(_slot(ranks, d, r)) for d in mld], mask, S.am)
                g.wait_ge(S.ho, EO)
                n += _send(g, T, topo, T.od[:], dests, [slot_o(_slot(ranks, d, r)) for d in dests], mask, arr(r))
                g.wait_ge(S.sent, n)
        return

    v, sc, pe, sy = g.vector, g.scalar, g.tensor, g.sync
    Exp = ActivationFunctionType.Exp
    mult, add = AluOpType.mult, AluOpType.add
    direct, helpers = _plan(ranks, topo, core)
    hcores = [h for h, _d in helpers]
    dgp = lambda p: T.dg[:, p * 128:(p + 1) * 128]
    m_all = T.mls[:, 0:NR * MW:MW]
    l_all = T.mls[:, 1:NR * MW:MW]
    n_am = (NR - 1) * ENG
    out_eng = topo.mask(core, direct[0])
    in_eng = topo.mask(core, hcores[0]) & ~out_eng
    dmask = _take(out_eng, ENG)

    sy.dma_start(T.od[:], T.o[:]).then_inc(S.ldd, 16)
    sc.dma_start(T.md[:], T.ml[:]).then_inc(S.ldmd, 16)
    sc.dma_start(T.z[:, 4:6], T.ml[:]).then_inc(S.ldm, 16)

    nxt = direct[0]
    nh = len(_plan(ranks, topo, nxt)[1])
    c0, wid = _share(nh, nh + 1)
    _make_share(g, T, T.idx[:, 0:wid], c0, wid)
    sent = _send(g, T, topo, T.idx[:, 0:wid], [nxt], [T.dif[:, c0:c0 + wid]], dmask, S.idr)

    v.memset(T.z[:, 2:3], BIG).then_inc(S.ms, 1)
    v.memset(T.z[:, 3:4], -BIG).then_inc(S.ms, 1)
    v.memset(T.z[:, 8:12], 1.0).then_inc(S.ms, 1)
    v.memset(T.z[:, 12:16], -1.0).then_inc(S.ms, 1)
    v.memset(T.z[:, 16:20], 0.0).then_inc(S.ms, 1)

    mlds = _ml_dests(ranks, topo, core)
    first = sorted(range(len(hcores)), key=lambda k: (-len(mlds[k]), k))
    g.wait_ge(S.ldmd, 16)
    g.remote_dma_fused([RemoteDMATransfer(dst_ids=[_id(topo, hcores[k]) for k in first[e::EM]],
                                          dma_engine_mask=_nth(in_eng, e), remote_sem=S.hm, srcs=[T.md[:]],
                                          dsts=[T.md[:] for _k in first[e::EM]], alu_op=0)
                        for e in range(EM)], local_sem=S.sent)
    sent += EM
    g.sem_inc(S.go, 1)
    sy.wait_ge(S.go, 1)
    sy.dma_start(slot_o(0), T.o[:]).then_inc(S.ldo, 16)
    g.wait_ge(S.ldd, 16)
    for group in ([h for h, ds in helpers if not topo.may_write(core, ds[0])],
                  [h for h, ds in helpers if topo.may_write(core, ds[0])]):
        sent += _send(g, T, topo, T.od[:], group, [T.od[:] for _h in group], _take(in_eng, EO), S.ho)
    sent += _send(g, T, topo, T.od[:], direct, [slot_o(_slot(ranks, d, core)) for d in direct], dmask, arr(core))

    v.wait_ge(S.ms, 5)
    v.wait_ge(S.ldm, 16)
    v.tensor_tensor_scan(T.hq[:, 0:4], T.z[:, 4:20:4], T.z[:, 2:6], 1.0, mult, add).then_inc(S.pk, 1)
    sc.wait_ge(S.pk, 1)
    sc.activation(T.eo[:, 0:1], T.hq[:, 2:3], Exp).then_inc(S.xo, 1)
    v.wait_ge(S.pk, 1)
    v.tensor_copy(T.mls[:, 0:1], T.hq[:, 1:2]).then_inc(S.own, 1)
    v.wait_ge(S.xo, 1)
    v.tensor_tensor(T.mls[:, 1:2], T.hq[:, 3:4], T.eo[:, 0:1], mult).then_inc(S.own, 1)
    v.wait_ge(S.idr, ENG * (len(helpers) + 1))
    v.tensor_scalar(T.ident[:], T.dif[:], 0.0, None, AluOpType.is_equal).then_inc(S.ids, 1)
    v.tensor_scalar(T.ido[:], T.dif[:], 0.0, T.eo[:, 0:1], AluOpType.is_equal, mult).then_inc(S.ids, 1)

    v.wait_ge(S.own, 2)
    v.wait_ge(S.am, n_am)
    v.tensor_reduce(T.nm[:, 0:1], m_all, AxisListType.X, AluOpType.max, negate=True).then_inc(S.rm, 1)
    sc.wait_ge(S.own, 2)
    sc.wait_ge(S.am, n_am)
    sc.wait_ge(S.rm, 1)
    sc.activation(T.f[:, 0:NR], m_all, Exp, bias=T.nm[:, 0:1]).then_inc(S.xf, 1)
    v.wait_ge(S.xf, 1)
    v.wait_ge(S.ids, 2)

    order = [core] + sorted([s for s in ranks if s != core], key=lambda s: _when(ranks, topo, s, core))
    last = len(order) - 1
    for k, s in enumerate(order):
        p = _slot(ranks, core, s)
        v.tensor_scalar(dgp(p), T.ido[:] if s == core else T.ident[:], T.f[:, p:p + 1], None,
                        mult).then_inc(S["d%d" % p], 1)
        if k == 2:
            v.tensor_tensor(T.fl[:, 0:NR], T.f[:, 0:NR], l_all, mult).then_inc(S.fls, 1)
        if k == 4:
            v.wait_ge(S.fls, 1)
            v.tensor_reduce(T.den[:, 0:1], T.fl[:, 0:NR], AxisListType.X, add).then_inc(S.dns, 1)
        if k == last:
            v.wait_ge(S.dns, 1)
            v.reciprocal(T.rden[:, 0:1], T.den[:, 0:1]).then_inc(S.rcs, 1)
        pe.wait_ge(S["d%d" % p], 1)
        if s == core:
            pe.wait_ge(S.ldo, 16)
        else:
            pe.wait_ge(arr(s), ENG)
        mm = pe.matmul(T.ps[:, 0:D], dgp(p), slot_o(p), k == 0, k == last)
        if k == last:
            mm.then_inc(S.pe1, 1)
    v.wait_ge(S.rcs, 1)
    v.wait_ge(S.pe1, 1)
    v.tensor_scalar(T.ysb[:], T.ps[:, 0:D], T.rden[:, 0:1], None, mult).then_inc(S.yv, 1)
    sy.wait_ge(S.yv, 1)
    sy.dma_start(T.y[:], T.ysb[:]).then_inc(S.st, 16)
    sy.wait_ge(S.st, 16)
    g.wait_ge(S.sent, sent)
